import numpy as np
import ml_dtypes


def mxq(x, axis, fmt="e4m3"):
    dtype, down = {"e4m3": (ml_dtypes.float8_e4m3fn, 7), "e5m2": (ml_dtypes.float8_e5m2, 14)}[fmt]
    v = np.moveaxis(np.asarray(x, np.float32).astype(ml_dtypes.bfloat16).astype(np.float64), axis, -1)
    blocks = v.reshape(v.shape[:-1] + (-1, 32))
    amax = np.abs(blocks).max(-1, keepdims=True)
    byte = np.maximum(np.where(amax > 0, np.frexp(amax)[1] - 1 + 127, 0) - down, 1)
    scale = np.exp2(byte - 127.0)
    codes = (blocks / scale).astype(np.float32).astype(dtype).astype(np.float64)
    return np.moveaxis((codes * scale).reshape(v.shape), -1, axis)


WIDE = False


def mx_kscale(k):
    if not WIDE:
        return np.ones(k)
    levels = np.array([10, -10, 5, -5, 0])
    if k % 512:
        return np.exp2(np.random.permutation(np.resize(levels, k // 32))).repeat(32)
    a = np.empty((k // 512, 16))
    for p in range(k // 512):
        a[p, :8] = np.random.permutation(np.resize(levels, 8))
        for g in range(8):
            far = levels[np.abs(levels - a[p, g]) >= 10]
            a[p, g + 8] = far[np.random.randint(len(far))]
    return np.exp2(a.ravel()).repeat(32)


def f64(x):
    return np.asarray(x).astype(np.float64)


def striped(idx):
    return np.tile(idx.reshape(-1, 16).T, (8, 1)).astype(np.uint16)


def unstriped(offs):
    return offs[:16].T.reshape(-1).astype(np.int64)


E2M1 = np.array([0.0, 0.5, 1.0, 1.5, 2.0, 3.0, 4.0, 6.0, -0.0, -0.5, -1.0, -1.5, -2.0, -3.0, -4.0, -6.0])


def pack_weight(w, fmt):
    k, n = w.shape
    w = f64(np.asarray(w, np.float32).astype(ml_dtypes.bfloat16)).reshape(k // 32, 32, n)
    amax = np.abs(w).max(1)
    if fmt == "e4m3":
        byte = np.frexp(amax)[1] - 1 + 127 - 7
    else:
        mant, ex = np.frexp(amax / 6.0)
        byte = np.where(mant > 0.5, ex, ex - 1) + 127
    byte = np.clip(np.where(amax > 0, byte, 1), 1, 254)
    scaled = (w * np.exp2(127.0 - byte)[:, None, :]).reshape(k, n).astype(np.float32)
    by_word = np.ascontiguousarray(scaled.reshape(k // 512, 128, 4, n).transpose(0, 1, 3, 2))
    if fmt == "e4m3":
        words = by_word.astype(ml_dtypes.float8_e4m3fn).view(np.uint8)
    else:
        c = by_word.astype(ml_dtypes.float4_e2m1fn).view(np.uint8) & 0xF
        words = (c[..., 0::2] | (c[..., 1::2] << 4)).reshape(k // 512, 128, 2 * n)
    return np.ascontiguousarray(words), np.ascontiguousarray(byte.astype(np.uint8).reshape(k // 512, 16, n))


def unpack_weight(words, scales, fmt):
    g, _, n = scales.shape
    words = np.ascontiguousarray(words).reshape(g, 128, n, -1)
    if fmt == "e4m3":
        vals = words.view(ml_dtypes.float8_e4m3fn).astype(np.float64)
    else:
        nib = np.empty((g, 128, n, 4), np.uint8)
        nib[..., 0::2] = words & 0xF
        nib[..., 1::2] = words >> 4
        vals = E2M1[nib]
    vals = vals * np.repeat(np.exp2(scales.astype(np.float64) - 127.0), 8, axis=1)[..., None]
    return vals.transpose(0, 1, 3, 2).reshape(g * 512, n)


def gelu(v):
    return 0.5 * v * (1.0 + np.tanh(np.sqrt(2.0 / np.pi) * (v + 0.044715 * v**3)))


def bf(x):
    return np.asarray(x, np.float32).astype(ml_dtypes.bfloat16)


def planes(Y):
    n, m = Y.shape
    b = f64(bf(Y)).reshape(n // 32, 32, m)
    amax = np.abs(b).max(1)
    byte = np.clip(np.where(amax > 0, np.frexp(amax)[1] - 1 + 127 - 7, 1), 1, 254)
    codes = (b * np.exp2(127.0 - byte)[:, None, :]).reshape(n, m).astype(np.float32).astype(ml_dtypes.float8_e4m3fn).view(np.uint8)
    words = codes.reshape(n // 512, 128, 4, m).transpose(0, 1, 3, 2)
    return np.ascontiguousarray(words), np.ascontiguousarray(byte.astype(np.uint8).reshape(n // 512, 16, m))


K, K2, T, TD, S, T2, P, H, N = 1024, 512, 2048, 1024, 512, 2048, 1024, 1024, 1024

def setup_inputs():
    n = np.random.standard_normal
    s, s2, u = mx_kscale(K)[:, None], mx_kscale(K2)[:, None], mx_kscale(H)[:, None]
    perm = np.random.permutation(T2)
    d = {}
    d["tab_words"], d["tab_scales"] = pack_weight(n((K, T)) * s, "e4m3")
    d["tab2_words"], d["tab2_scales"] = pack_weight(n((K2, TD)) * s2, "e4m3")
    d["offs"] = striped(np.random.permutation(T)[:S])
    d["offs2"] = striped(np.random.permutation(TD)[:S])
    d["offs3"] = striped(perm[:S])
    d["offs4"] = striped(perm[S:2 * S])
    d["offs5"] = striped(np.random.permutation(T2)[:P])
    d["w1"] = (1.5 * n((K, H)) / K ** 0.5 / s).astype(np.float32)
    d["w4_words"], d["w4_scales"] = pack_weight(0.55 * n((K2, H)) / K2 ** 0.5 / s2, "e2m1")
    d["w8_words"], d["w8_scales"] = pack_weight(n((H, N)) / H ** 0.5 / u * np.exp(0.8 * n((1, N))), "e4m3")
    d["page0"] = n((H, T2)).astype(np.float32)
    d["wg1"] = np.exp(0.3 * n((128, S))).astype(np.float32)
    d["wg2"] = np.exp(0.3 * n((128, S))).astype(np.float32)
    d["lim"] = (0.5 * n(H)).astype(np.float32)
    d["gx"] = (np.exp(0.3 * n(H)) * u[:, 0]).astype(np.float32)
    d["gs"] = np.exp(0.3 * n(N)).astype(np.float32)
    return d

def reference(tab_words, tab_scales, tab2_words, tab2_scales, offs, offs2, offs3, offs4, offs5, w1, w4_words, w4_scales, w8_words, w8_scales, page0, wg1, wg2, lim, gx, gs):
    v = unpack_weight(tab_words, tab_scales, "e4m3")[:, unstriped(offs)]
    v2 = unpack_weight(tab2_words, tab2_scales, "e4m3")[:, unstriped(offs2)]
    vib = mxq(f64(w1), 0, "e4m3").T @ v
    h1 = 0.5 * vib * (1.0 + np.tanh(0.7978845608 * (vib + 0.044715 * vib ** 3)))
    h2 = np.cos(unpack_weight(w4_words, w4_scales, "e2m1").T @ v2)
    page = f64(page0).copy()
    page[:, unstriped(offs3)] = np.tile(f64(wg1), (H // 128, 1)) * h1
    page[:, unstriped(offs4)] = np.tile(f64(wg2), (H // 128, 1)) * h2
    x = np.maximum(page[:, unstriped(offs5)], f64(lim)[:, None]) * f64(gx)[:, None]
    f = unpack_weight(w8_words, w8_scales, "e4m3").T @ mxq(x, 0, "e4m3")
    y = f + f64(gs)[:, None] * (f / (1.0 + np.exp(-f)))
    words, scales = planes(y)
    return y, words, scales

@@ -1,0 +1,360 @@
+import math
+from contextlib import ExitStack
+
+import concourse.mybir as mybir
+from concourse.masks import make_identity
+
+K, K2, T, TD, S, T2, PJ, H, N = 1024, 512, 2048, 1024, 512, 2048, 1024, 1024, 1024
+FLOPS = 2 * (K * H * S + K2 * H * S + H * N * PJ)
+
+F32 = mybir.dt.float32
+BF16 = mybir.dt.bfloat16
+I32 = mybir.dt.int32
+U32 = mybir.dt.uint32
+U16 = mybir.dt.uint16
+U8 = mybir.dt.uint8
+FP8X4 = mybir.dt.float8_e4m3fn_x4
+FP4X4 = mybir.dt.float4_e2m1fn_x4
+ACT = mybir.ActivationFunctionType
+ALU = mybir.AluOpType
+
+P = 128
+BANK = 512
+ROUNDER = 1.5 * 2.0**23
+
+
+def tile_list_gearbox_slot_features_kernel(
+    tc, tab_words, tab_scales, tab2_words, tab2_scales, offs, offs2, offs3, offs4, offs5,
+    w1, w4_words, w4_scales, w8_words, w8_scales, page0, wg1, wg2, lim, gx, gs, out_0, out_1, out_2,
+):
+    nc = tc.nc
+    with ExitStack() as ctx:
+        lists = ctx.enter_context(tc.tile_pool(name="lists", bufs=1))
+        sb = ctx.enter_context(tc.tile_pool(name="sb", bufs=1))
+        ring = ctx.enter_context(tc.tile_pool(name="ring", bufs=2))
+        psum = ctx.enter_context(tc.psum_pool(name="psum", bufs=1))
+
+        def held(name, shape, dtype, tag=None):
+            return sb.tile(shape, dtype, name=name, tag=tag or name, align_bytes=64)
+
+        def ringed(name, shape, dtype, tag):
+            return ring.tile(shape, dtype, name=name, tag=tag, align_bytes=64)
+
+        def bank(name, n):
+            return psum.tile([P, BANK], F32, name=name, tag=f"bank{n}")
+
+        def load_list(name, src):
+            t = lists.tile(list(src.shape), U16, name=name)
+            nc.sync.dma_start(t[:], src)
+            return t
+
+        def load_words(name, src, tag=None):
+            t = held(name, [P, src.shape[1]], I32, tag)
+            nc.sync.dma_start(out=t[:], in_=src.rearrange("p n t -> p (n t)").bitcast(I32))
+            return t
+
+        def load_scales(queue, plane, src):
+            rows = 4 * src.shape[0]
+            for q in range(4):
+                queue.dma_start(
+                    out=plane[32 * q : 32 * q + rows, :].bitcast(I32),
+                    in_=src[:, 4 * q : 4 * q + 4, :].bitcast(I32),
+                )
+
+        def load_page(i):
+            b, t = divmod(i, 4)
+            pg = held(f"page{i}", [P, T2], F32)
+            nc.sync.dma_start(out=pg[:], in_=page0.rearrange("(b p t) c -> b t p c", b=2, t=4)[b, t])
+            return pg
+
+        def load_gain(dst, src, t0, t1):
+            for q in range(4):
+                nc.sync.dma_start(
+                    out=dst[32 * q : 32 * q + 32, t0:t1, :],
+                    in_=src.rearrange("(p t) j -> p t j", t=4)[:, t0:t1, :],
+                )
+
+        def load_w1(a, b, tag):
+            raw = held(f"w1raw{a}{b}", [P, 4, BANK], F32, tag)
+            nc.sync.dma_start(
+                out=raw[:],
+                in_=w1[512 * a : 512 * (a + 1), 512 * b : 512 * (b + 1)].rearrange("(p j) c -> p j c", j=4),
+            )
+            return raw
+
+        def load_vec(name, src):
+            v = held(name, [P, 2, 4], F32)
+            nc.sync.dma_start(out=v[:], in_=src.rearrange("(b p t) -> p b t", b=2, t=4))
+            return v
+
+        t2s = held("t2s", [P, TD], U8, "w8d")
+        w4s = held("w4s", [P, H], U8)
+        tbs = held("tbs", [P, T], U8)
+        w8s = held("w8s", [P, N], U8)
+        nc.vector.memset(t2s[:].bitcast(I32), 0)
+        nc.vector.memset(w4s[:].bitcast(I32), 0)
+        warm = held("warm", [P, 4], F32)
+        nc.vector.memset(warm[:, 0:1], 0.0)
+        nc.scalar.activation(out=warm[:, 1:2], in_=warm[:, 0:1], func=ACT.Sin)
+        o2 = load_list("o2", offs2)
+        t2w = load_words("t2w", tab2_words[0])
+        load_scales(nc.sync, t2s, tab2_scales)
+        w4w = held("w4w", [P, 2 * H], U8)
+        nc.sync.dma_start(out=w4w[:].bitcast(I32), in_=w4_words[0].bitcast(I32))
+        w8raw = held("w8raw", [P, 2, N], I32, "big3")
+        nc.sync.dma_start(out=w8raw[:], in_=w8_words.rearrange("a p n t -> p a (n t)").bitcast(I32))
+        load_scales(nc.sync, w4s, w4_scales)
+        nc.vector.memset(tbs[:].bitcast(I32), 0)
+        nc.gpsimd.memset(w8s[:].bitcast(I32), 0)
+        load_scales(nc.gpsimd, w8s, w8_scales)
+        ident = held("ident", [P, P], F32)
+        make_identity(nc, ident[:])
+        o1 = load_list("o1", offs)
+        tbw = [load_words("tbw0", tab_words[0]), load_words("tbw1", tab_words[1])]
+        load_scales(nc.sync, tbs, tab_scales)
+
+        v2w = held("v2w", [P, S], U32)
+        v2s = held("v2s", [P, S], U8)
+        nc.vector.tensor_copy(v2w[:], t2w[:].bitcast(U32).indirect(o2[:]))
+        nc.vector.tensor_copy(v2s[:], t2s[:].indirect(o2[:]))
+
+        w8d = held("w8d", [P, 2, N], I32)
+        for a in range(2):
+            nc.vector.tensor_copy(
+                out=w8d[:, a, :].rearrange("p (g t q) -> p g q t", g=2, t=4),
+                in_=w8raw[:, a, :].rearrange("p (g q t) -> p g q t", g=2, t=4),
+            )
+        vw = held("vw", [P, 2, S], U32)
+        vs = held("vs", [P, S], U8)
+        for a in range(2):
+            nc.vector.tensor_copy(vw[:, a, :], tbw[a][:].bitcast(U32).indirect(o1[:]))
+        nc.vector.tensor_copy(vs[:], tbs[:].indirect(o1[:]))
+        w8sd = held("w8sd", [P, N], U8)
+        nc.vector.tensor_copy(
+            out=w8sd[:].rearrange("p (g t q) -> p g q t", g=2, t=4),
+            in_=w8s[:].rearrange("p (g q t) -> p g q t", g=2, t=4),
+        )
+
+        o4 = load_list("o4", offs4)
+        wg2d = held("wg2d", [P, 4, S], F32)
+        wg1d = held("wg1d", [P, 4, S], F32)
+        load_gain(wg2d, wg2, 0, 2)
+        pages = [load_page(0), load_page(1)]
+        load_gain(wg2d, wg2, 2, 4)
+        pages += [load_page(2), load_page(3)]
+        lim_v = load_vec("lim_v", lim)
+        gx_v = load_vec("gx_v", gx)
+        gs_v = load_vec("gs_v", gs)
+        pages.append(load_page(4))
+        pages.append(load_page(5))
+        w1raw = {(0, 0): load_w1(0, 0, "big0")}
+        w1raw[(1, 0)] = load_w1(1, 0, "big1")
+        pages.append(load_page(6))
+        pages.append(load_page(7))
+        o3 = load_list("o3", offs3)
+        o5 = load_list("o5", offs5)
+        load_gain(wg1d, wg1, 0, 2)
+        w1raw[(0, 1)] = load_w1(0, 1, "big2")
+        load_gain(wg1d, wg1, 2, 4)
+        w1raw[(1, 1)] = load_w1(1, 1, "big3")
+
+        def turns(b):
+            u = held(f"turns{b}", [P, 4, 4, P], F32)
+            for jt in range(4):
+                z = bank(f"z{b}{jt}", jt)
+                nc.tensor.matmul_mx(
+                    out=z[:],
+                    lhsT=v2w[:, jt * P : (jt + 1) * P].bitcast(FP8X4),
+                    lhsT_scale=v2s[:, jt * P : (jt + 1) * P],
+                    rhs=w4w[:, 1024 * b : 1024 * (b + 1)].bitcast(FP4X4),
+                    rhs_scale=w4s[:, 512 * b : 512 * (b + 1)],
+                    start=True,
+                    stop=True,
+                )
+                nc.scalar.activation(
+                    out=u[:, jt, :, :],
+                    in_=z[:].rearrange("p (q t) -> p t q", t=4),
+                    func=ACT.Copy,
+                    scale=1.0 / (2.0 * math.pi),
+                    bias=0.25,
+                )
+            return u
+
+        def cos_rows(i, u):
+            t = i % 4
+            whole = ringed(f"whole{i}", [P, 4, P], U32, "ka")
+            nc.scalar.activation(out=whole[:], in_=u[:, :, t, :], func=ACT.Copy, scale=1.0, bias=ROUNDER)
+            minus = ringed(f"minus{i}", [P, 4, P], F32, "kb")
+            nc.scalar.activation(out=minus[:], in_=whole[:], func=ACT.Copy, scale=-1.0, bias=ROUNDER)
+            frac = bank(f"frac{i}", 4 + i % 2)
+            for jt in range(4):
+                cols = frac[:, jt * P : (jt + 1) * P]
+                nc.tensor.matmul(cols, u[:, jt, t, :], ident[:], start=True, stop=False, is_transpose=True)
+                nc.tensor.matmul(cols, minus[:, jt, :], ident[:], start=False, stop=True, is_transpose=True)
+            h = held(f"h2_{i}", [P, S], F32, f"h{i}")
+            nc.scalar.activation(out=h[:], in_=frac[:], func=ACT.Sin, scale=2.0 * math.pi)
+            if i == 7:
+                nc.scalar.activation(out=warm[:, 2:3], in_=h[:, 0:1], func=ACT.Gelu_apprx_tanh)
+            return h
+
+        def put(i, h, gain, offsets):
+            nc.vector.tensor_tensor(pages[i][:].indirect(offsets[:]), h[:], gain[:, i % 4, :], ALU.mult)
+
+        w1c = held("w1c", [P, 2, H], U32)
+        w1s = held("w1s", [P, 2, H], U8)
+
+        def round_w1(a, b):
+            grouped = ringed(f"w1g{a}{b}", [P, 4 * BANK], BF16, "grp")
+            nc.scalar.copy(
+                out=grouped[:].rearrange("p (t m j) -> p m t j", t=4, j=4),
+                in_=w1raw[(a, b)][:].rearrange("p j (m t) -> p m t j", t=4),
+            )
+            return grouped
+
+        def quant_w1(a, b, grouped):
+            cols = slice(512 * b, 512 * (b + 1))
+            nc.vector.quantize_mx(out=w1c[:, a, cols].bitcast(FP8X4), scales=w1s[:, a, cols], in_=grouped[:])
+
+        for b in range(2):
+            u = turns(b)
+            for t in range(4):
+                i = 4 * b + t
+                put(i, cos_rows(i, u), wg2d, o4)
+                if i in (5, 6):
+                    quant_w1(i - 5, 0, round_w1(i - 5, 0))
+
+        gx_lim = held("gx_lim", [P, 8], F32)
+        lim_f = lim_v[:].rearrange("p b t -> p (b t)")
+        gx_f = gx_v[:].rearrange("p b t -> p (b t)")
+        gs_f = gs_v[:].rearrange("p b t -> p (b t)")
+        nc.gpsimd.tensor_tensor(gx_lim[:], lim_f, gx_f, ALU.mult)
+
+        def gelu_rows(i):
+            vib = bank(f"vib{i}", 6 + i % 2)
+            cols = slice(P * i, P * (i + 1))
+            for a in range(2):
+                nc.tensor.matmul_mx(
+                    out=vib[:],
+                    lhsT=w1c[:, a, cols].bitcast(FP8X4),
+                    lhsT_scale=w1s[:, a, cols],
+                    rhs=vw[:, a, :].bitcast(FP8X4),
+                    rhs_scale=vs[4 * a : P, :],
+                    start=(a == 0),
+                    stop=(a == 1),
+                )
+            h = held(f"h1_{i}", [P, S], F32, f"h{(i + 1) % 4}")
+            nc.scalar.activation(out=h[:], in_=vib[:], func=ACT.Gelu_apprx_tanh)
+            if i == 7:
+                nc.scalar.activation(out=warm[:, 3:4], in_=h[:, 0:1], func=ACT.Silu)
+            return h
+
+        xc = held("xc", [P, 2 * PJ], U32, "turns0")
+        xs = [held(f"xs{a}", [P, PJ], U8) for a in range(2)]
+
+        def weave(engine, dst, src):
+            dst_v = dst.rearrange("p (c i t) -> p c t i", i=4, t=4)
+            src_v = src.rearrange("p t (c i) -> p c t i", i=4)
+            if engine == "scalar":
+                nc.scalar.copy(out=dst_v, in_=src_v)
+            else:
+                nc.vector.tensor_copy(out=dst_v, in_=src_v)
+
+        def quant_x(a, c, woven):
+            nc.vector.quantize_mx(
+                out=xc[:, a * PJ + c * BANK : a * PJ + (c + 1) * BANK].bitcast(FP8X4),
+                scales=xs[a][:, c * BANK : (c + 1) * BANK],
+                in_=woven,
+            )
+
+        def bound_on_scalar(i, got, dsts):
+            nc.scalar.activation(out=got, in_=got, func=ACT.Relu, bias=neg_lim[:, i : i + 1])
+            width = got.shape[1] // len(dsts)
+            for c, dst in enumerate(dsts):
+                nc.scalar.activation(
+                    out=dst, in_=got[:, c * width : (c + 1) * width], func=ACT.Identity,
+                    scale=gx_f[:, i : i + 1], bias=gx_lim[:, i : i + 1],
+                )
+
+        h1 = [gelu_rows(i) for i in range(3)]
+        for a in range(2):
+            quant_w1(a, 1, round_w1(a, 1))
+        xb0 = held("xb0", [P, 4 * PJ + 16], BF16, "big3")
+        neg_lim = xb0[:, 4 * PJ :].bitcast(F32)
+        nc.gpsimd.tensor_scalar(neg_lim, lim_f, -1.0, 0.0, ALU.mult, ALU.add)
+        xb = xb0[:, : 4 * PJ].rearrange("p (t j) -> p t j", t=4)
+        xw0 = held("xw0", [P, 4 * PJ], BF16, "big0")
+        xw1 = [held(f"xw1{c}", [P, BANK, 4], BF16, f"big{1 + c}") for c in range(2)]
+        for i in range(6):
+            put(i, h1[i], wg1d, o3)
+            got = held(f"got{i}", [P, PJ], F32, f"h{i % 4}")
+            nc.vector.tensor_copy(got[:], pages[i][:].indirect(o5[:]))
+            bound_on_scalar(i, got[:], [xb[:, i, :]] if i < 4 else [w[:, :, i - 4] for w in xw1])
+            if i + 3 < 8:
+                h1.append(gelu_rows(i + 3))
+            if i == 3:
+                for c in range(2):
+                    weave("scalar", xw0[:, c * 2048 : (c + 1) * 2048], xb[:, :, c * BANK : (c + 1) * BANK])
+                    quant_x(0, c, xw0[:, c * 2048 : (c + 1) * 2048])
+
+        put(6, h1[6], wg1d, o3)
+        for c in range(2):
+            got = held(f"got6{c}", [P, BANK], F32, f"h{4 + c}")
+            nc.vector.tensor_copy(got[:], pages[6][:].indirect(o5[:, 32 * c : 32 * (c + 1)]))
+            bound_on_scalar(6, got[:], [xw1[c][:, :, 2]])
+        put(7, h1[7], wg1d, o3)
+        gx_late = held("gx_late", [P, 1], F32, "h5")
+        nc.scalar.copy(out=gx_late[:], in_=gx_f[:, 7:8])
+        for c in range(2):
+            got = held(f"got7{c}", [P, BANK], F32, "h4" if c == 0 else "big1")
+            nc.vector.tensor_copy(got[:], pages[7][:].indirect(o5[:, 32 * c : 32 * (c + 1)]))
+            nc.vector.tensor_scalar(
+                xw1[c][:, :, 3], got[:], lim_f[:, 7:8], gx_f[:, 7:8] if c == 0 else gx_late[:], ALU.max, ALU.mult
+            )
+            quant_x(1, c, xw1[c][:].rearrange("p j t -> p (j t)"))
+
+        yc = held("yc", [P, 2 * PJ], U32, "tbw0")
+        ys = held("ys", [P, PJ], U8)
+        out_rows = out_0.rearrange("(g p t) j -> g p t j", g=2, t=4)
+        pending = []
+
+        def finish(g, c, woven):
+            cols = slice(c * BANK, (c + 1) * BANK)
+            words = yc[:, g * PJ + c * BANK : g * PJ + (c + 1) * BANK]
+            nc.vector.quantize_mx(out=words.bitcast(FP8X4), scales=ys[4 * g : P, cols], in_=woven[:])
+            nc.sync.dma_start(
+                out=out_1[g].rearrange("p m t -> p (m t)").bitcast(I32)[:, cols], in_=words.bitcast(I32)
+            )
+
+        for c in range(2):
+            for g in range(2):
+                y = held(f"y{g}{c}", [P, 4, BANK], F32, f"page{2 * c + g}")
+                for t in range(4):
+                    n = 4 * g + t
+                    f = bank(f"f{c}{n}", n)
+                    cols = slice(P * n, P * (n + 1))
+                    for a in range(2):
+                        nc.tensor.matmul_mx(
+                            out=f[:],
+                            lhsT=w8d[:, a, cols].bitcast(FP8X4),
+                            lhsT_scale=w8sd[4 * a : P, cols],
+                            rhs=xc[:, a * PJ + c * BANK : a * PJ + (c + 1) * BANK].bitcast(FP8X4),
+                            rhs_scale=xs[a][:, c * BANK : (c + 1) * BANK],
+                            start=(a == 0),
+                            stop=(a == 1),
+                        )
+                    s = ringed(f"silu{c}{n}", [P, BANK], F32, "ka" if n % 2 == 0 else "kb")
+                    nc.scalar.activation(out=s[:], in_=f[:], func=ACT.Silu)
+                    nc.vector.scalar_tensor_tensor(y[:, t, :], s[:], gs_f[:, n : n + 1], f[:], ALU.mult, ALU.add)
+                    if t == 1 and pending:
+                        finish(*pending.pop())
+                nc.sync.dma_start(out=out_rows[g][:, :, c * BANK : (c + 1) * BANK], in_=y[:])
+                woven = ringed(f"yw{g}{c}", [P, 4 * BANK], BF16, "grp")
+                last = c == 1 and g == 1
+                weave("vector" if last else "scalar", woven[:], y[:])
+                pending.append((g, c, woven))
+        finish(*pending.pop())
+        for q in range(4):
+            nc.sync.dma_start(
+                out=out_2[:, 4 * q : 4 * q + 4, :].bitcast(I32),
+                in_=ys[32 * q : 32 * q + 8, :].bitcast(I32),
+            )

@@ -20,6 +20,7 @@ ALU = mybir.AluOpType
 
 P = 128
 BANK = 512
+VECTOR_SHARE = (0, 192, 192, 352)
 ROUNDER = 1.5 * 2.0**23
 
 
@@ -110,7 +111,7 @@ def tile_list_gearbox_slot_features_kernel(
         ident = held("ident", [P, P], F32)
         make_identity(nc, ident[:])
         o1 = load_list("o1", offs)
-        tbw = [load_words("tbw0", tab_words[0]), load_words("tbw1", tab_words[1])]
+        tbw = [load_words("tbw0", tab_words[0])]
         load_scales(nc.sync, tbs, tab_scales)
 
         v2w = held("v2w", [P, S], U32)
@@ -126,10 +127,9 @@ def tile_list_gearbox_slot_features_kernel(
             )
         vw = held("vw", [P, 2, S], U32)
         vs = held("vs", [P, S], U8)
-        for a in range(2):
-            nc.vector.tensor_copy(vw[:, a, :], tbw[a][:].bitcast(U32).indirect(o1[:]))
+        nc.vector.tensor_copy(vw[:, 0, :], tbw[0][:].bitcast(U32).indirect(o1[:]))
         nc.vector.tensor_copy(vs[:], tbs[:].indirect(o1[:]))
-        w8sd = held("w8sd", [P, N], U8)
+        w8sd = held("w8sd", [P, N], U8, "tbs")
         nc.vector.tensor_copy(
             out=w8sd[:].rearrange("p (g t q) -> p g q t", g=2, t=4),
             in_=w8s[:].rearrange("p (g q t) -> p g q t", g=2, t=4),
@@ -141,7 +141,9 @@ def tile_list_gearbox_slot_features_kernel(
         load_gain(wg2d, wg2, 0, 2)
         pages = [load_page(0), load_page(1)]
         load_gain(wg2d, wg2, 2, 4)
-        pages += [load_page(2), load_page(3)]
+        pages.append(load_page(2))
+        tbw.append(load_words("tbw1", tab_words[1]))
+        pages.append(load_page(3))
         lim_v = load_vec("lim_v", lim)
         gx_v = load_vec("gx_v", gx)
         gs_v = load_vec("gs_v", gs)
@@ -189,8 +191,10 @@ def tile_list_gearbox_slot_features_kernel(
             frac = bank(f"frac{i}", 4 + i % 2)
             for jt in range(4):
                 cols = frac[:, jt * P : (jt + 1) * P]
-                nc.tensor.matmul(cols, u[:, jt, t, :], ident[:], start=True, stop=False, is_transpose=True)
-                nc.tensor.matmul(cols, minus[:, jt, :], ident[:], start=False, stop=True, is_transpose=True)
+                nc.tensor.matmul(cols, u[:, jt, t, :], ident[:], start=(jt == 0), stop=False, is_transpose=True)
+            for jt in range(4):
+                cols = frac[:, jt * P : (jt + 1) * P]
+                nc.tensor.matmul(cols, minus[:, jt, :], ident[:], start=False, stop=(jt == 3), is_transpose=True)
             h = held(f"h2_{i}", [P, S], F32, f"h{i}")
             nc.scalar.activation(out=h[:], in_=frac[:], func=ACT.Sin, scale=2.0 * math.pi)
             if i == 7:
@@ -220,6 +224,8 @@ def tile_list_gearbox_slot_features_kernel(
             for t in range(4):
                 i = 4 * b + t
                 put(i, cos_rows(i, u), wg2d, o4)
+                if i == 2:
+                    nc.vector.tensor_copy(vw[:, 1, :], tbw[1][:].bitcast(U32).indirect(o1[:]))
                 if i in (5, 6):
                     quant_w1(i - 5, 0, round_w1(i - 5, 0))
 
@@ -342,15 +348,20 @@ def tile_list_gearbox_slot_features_kernel(
                             start=(a == 0),
                             stop=(a == 1),
                         )
-                    s = ringed(f"silu{c}{n}", [P, BANK], F32, "ka" if n % 2 == 0 else "kb")
+                    if n < 4:
+                        s = ringed(f"silu{c}{n}", [P, BANK], F32, "ka" if n % 2 == 0 else "kb")
+                    else:
+                        s = held(f"silu{c}{n}", [P, BANK], F32, f"h{n - 4}")
                     nc.scalar.activation(out=s[:], in_=f[:], func=ACT.Silu)
                     nc.vector.scalar_tensor_tensor(y[:, t, :], s[:], gs_f[:, n : n + 1], f[:], ALU.mult, ALU.add)
                     if t == 1 and pending:
                         finish(*pending.pop())
                 nc.sync.dma_start(out=out_rows[g][:, :, c * BANK : (c + 1) * BANK], in_=y[:])
                 woven = ringed(f"yw{g}{c}", [P, 4 * BANK], BF16, "grp")
-                last = c == 1 and g == 1
-                weave("vector" if last else "scalar", woven[:], y[:])
+                share = VECTOR_SHARE[2 * c + g]
+                if share:
+                    weave("vector", woven[:, : 4 * share], y[:, :, :share])
+                weave("scalar", woven[:, 4 * share :], y[:, :, share:])
                 pending.append((g, c, woven))
         finish(*pending.pop())
         for q in range(4):

@@ -229,11 +229,9 @@ def tile_list_gearbox_slot_features_kernel(
                 if i in (5, 6):
                     quant_w1(i - 5, 0, round_w1(i - 5, 0))
 
-        gx_lim = held("gx_lim", [P, 8], F32)
         lim_f = lim_v[:].rearrange("p b t -> p (b t)")
         gx_f = gx_v[:].rearrange("p b t -> p (b t)")
         gs_f = gs_v[:].rearrange("p b t -> p (b t)")
-        nc.gpsimd.tensor_tensor(gx_lim[:], lim_f, gx_f, ALU.mult)
 
         def gelu_rows(i):
             vib = bank(f"vib{i}", 6 + i % 2)
@@ -248,7 +246,7 @@ def tile_list_gearbox_slot_features_kernel(
                     start=(a == 0),
                     stop=(a == 1),
                 )
-            h = held(f"h1_{i}", [P, S], F32, f"h{(i + 1) % 4}")
+            h = held(f"h1_{i}", [P, S], F32, f"h{i % 4}")
             nc.scalar.activation(out=h[:], in_=vib[:], func=ACT.Gelu_apprx_tanh)
             if i == 7:
                 nc.scalar.activation(out=warm[:, 3:4], in_=h[:, 0:1], func=ACT.Silu)
@@ -272,51 +270,67 @@ def tile_list_gearbox_slot_features_kernel(
                 in_=woven,
             )
 
-        def bound_on_scalar(i, got, dsts):
+        def bound_on_scalar(i, got, dsts, floor):
             nc.scalar.activation(out=got, in_=got, func=ACT.Relu, bias=neg_lim[:, i : i + 1])
             width = got.shape[1] // len(dsts)
             for c, dst in enumerate(dsts):
                 nc.scalar.activation(
                     out=dst, in_=got[:, c * width : (c + 1) * width], func=ACT.Identity,
-                    scale=gx_f[:, i : i + 1], bias=gx_lim[:, i : i + 1],
+                    scale=gx_f[:, i : i + 1], bias=floor[:],
                 )
 
-        h1 = [gelu_rows(i) for i in range(3)]
+        def join_pairs(engine, dst, pairs):
+            dst_v = dst.bitcast(F32).rearrange("p (j u) -> p j u", u=2)
+            src_v = pairs.rearrange("p u j e -> p u (j e)").bitcast(F32).rearrange("p u j -> p j u")
+            if engine == "scalar":
+                nc.scalar.copy(out=dst_v, in_=src_v)
+            else:
+                nc.vector.tensor_copy(out=dst_v, in_=src_v)
+
+        h1 = [gelu_rows(i) for i in range(4)]
         for a in range(2):
             quant_w1(a, 1, round_w1(a, 1))
-        xb0 = held("xb0", [P, 4 * PJ + 16], BF16, "big3")
-        neg_lim = xb0[:, 4 * PJ :].bitcast(F32)
-        nc.gpsimd.tensor_scalar(neg_lim, lim_f, -1.0, 0.0, ALU.mult, ALU.add)
-        xb = xb0[:, : 4 * PJ].rearrange("p (t j) -> p t j", t=4)
+        xp0_tile = held("xp0", [P, 4 * PJ + 16], BF16, "big3")
+        neg_lim = xp0_tile[:, 4 * PJ :].bitcast(F32)
+        nc.scalar.activation(out=neg_lim, in_=lim_f, func=ACT.Copy, scale=-1.0)
+        neg_gx = held("neg_gx", [P, 8], F32)
+        nc.gpsimd.tensor_scalar(neg_gx[:], gx_f, -1.0, 0.0, ALU.mult, ALU.add)
+        xp0 = xp0_tile[:, : 4 * PJ].rearrange("p (u j e) -> p u j e", u=2, e=2)
         xw0 = held("xw0", [P, 4 * PJ], BF16, "big0")
-        xw1 = [held(f"xw1{c}", [P, BANK, 4], BF16, f"big{1 + c}") for c in range(2)]
-        for i in range(6):
+        xp1 = [held(f"xp1{c}", [P, 2, BANK, 2], BF16, f"big{1 + c}") for c in range(2)]
+        for i in range(7):
+            u, e = divmod(i % 4, 2)
             put(i, h1[i], wg1d, o3)
-            got = held(f"got{i}", [P, PJ], F32, f"h{i % 4}")
-            nc.vector.tensor_copy(got[:], pages[i][:].indirect(o5[:]))
-            bound_on_scalar(i, got[:], [xb[:, i, :]] if i < 4 else [w[:, :, i - 4] for w in xw1])
-            if i + 3 < 8:
-                h1.append(gelu_rows(i + 3))
+            floor = held(f"floor{i}", [P, 1], F32, f"h{i % 4}")
+            nc.scalar.activation(out=floor[:], in_=neg_lim[:, i : i + 1], func=ACT.Copy, scale=neg_gx[:, i : i + 1])
+            got = ringed(f"got{i}", [P, PJ], F32, "got")
+            if i < 6:
+                nc.vector.tensor_copy(got[:], pages[i][:].indirect(o5[:]))
+                bound_on_scalar(i, got[:], [xp0[:, u, :, e]] if i < 4 else [w[:, u, :, e] for w in xp1], floor)
+            else:
+                for c in range(2):
+                    half = got[:, c * BANK : (c + 1) * BANK]
+                    nc.vector.tensor_copy(half, pages[i][:].indirect(o5[:, 32 * c : 32 * (c + 1)]))
+                    bound_on_scalar(i, half, [xp1[c][:, u, :, e]], floor)
+                    nc.scalar.copy(out=got[:, c * BANK : c * BANK + 1], in_=gx_f[:, 7:8])
+            if i < 4:
+                h1.append(gelu_rows(i + 4))
             if i == 3:
                 for c in range(2):
-                    weave("scalar", xw0[:, c * 2048 : (c + 1) * 2048], xb[:, :, c * BANK : (c + 1) * BANK])
+                    join_pairs("scalar", xw0[:, c * 2048 : (c + 1) * 2048], xp0[:, :, c * BANK : (c + 1) * BANK, :])
                     quant_x(0, c, xw0[:, c * 2048 : (c + 1) * 2048])
 
-        put(6, h1[6], wg1d, o3)
-        for c in range(2):
-            got = held(f"got6{c}", [P, BANK], F32, f"h{4 + c}")
-            nc.vector.tensor_copy(got[:], pages[6][:].indirect(o5[:, 32 * c : 32 * (c + 1)]))
-            bound_on_scalar(6, got[:], [xw1[c][:, :, 2]])
+        got6 = got
         put(7, h1[7], wg1d, o3)
-        gx_late = held("gx_late", [P, 1], F32, "h5")
-        nc.scalar.copy(out=gx_late[:], in_=gx_f[:, 7:8])
         for c in range(2):
-            got = held(f"got7{c}", [P, BANK], F32, "h4" if c == 0 else "big1")
+            got = ringed("got70", [P, BANK], F32, "got") if c == 0 else held("got71", [P, BANK], F32, "tbw1")
             nc.vector.tensor_copy(got[:], pages[7][:].indirect(o5[:, 32 * c : 32 * (c + 1)]))
             nc.vector.tensor_scalar(
-                xw1[c][:, :, 3], got[:], lim_f[:, 7:8], gx_f[:, 7:8] if c == 0 else gx_late[:], ALU.max, ALU.mult
+                xp1[c][:, 1, :, 1], got[:], lim_f[:, 7:8], got6[:, c * BANK : c * BANK + 1], ALU.max, ALU.mult
             )
-            quant_x(1, c, xw1[c][:].rearrange("p j t -> p (j t)"))
+            xw1 = held(f"xw1{c}", [P, 4 * BANK], BF16, "tbw1" if c == 0 else "turns1")
+            join_pairs("vector", xw1[:], xp1[c][:])
+            quant_x(1, c, xw1[:])
 
         yc = held("yc", [P, 2 * PJ], U32, "tbw0")
         ys = held("ys", [P, PJ], U8)
@@ -354,9 +368,9 @@ def tile_list_gearbox_slot_features_kernel(
                         s = held(f"silu{c}{n}", [P, BANK], F32, f"h{n - 4}")
                     nc.scalar.activation(out=s[:], in_=f[:], func=ACT.Silu)
                     nc.vector.scalar_tensor_tensor(y[:, t, :], s[:], gs_f[:, n : n + 1], f[:], ALU.mult, ALU.add)
+                    nc.sync.dma_start(out=out_rows[g][:, t, c * BANK : (c + 1) * BANK], in_=y[:, t, :])
                     if t == 1 and pending:
                         finish(*pending.pop())
-                nc.sync.dma_start(out=out_rows[g][:, :, c * BANK : (c + 1) * BANK], in_=y[:])
                 woven = ringed(f"yw{g}{c}", [P, 4 * BANK], BF16, "grp")
                 share = VECTOR_SHARE[2 * c + g]
                 if share:
@@ -365,7 +379,7 @@ def tile_list_gearbox_slot_features_kernel(
                 pending.append((g, c, woven))
         finish(*pending.pop())
         for q in range(4):
-            nc.sync.dma_start(
+            nc.scalar.dma_start(
                 out=out_2[:, 4 * q : 4 * q + 4, :].bitcast(I32),
                 in_=ys[32 * q : 32 * q + 8, :].bitcast(I32),
             )

@@ -69,7 +69,7 @@ def tile_list_gearbox_slot_features_kernel(
             return pg
 
         def load_gain(dst, src, t0, t1):
-            for q in range(4):
+            for q in (0, 2, 1, 3):
                 nc.sync.dma_start(
                     out=dst[32 * q : 32 * q + 32, t0:t1, :],
                     in_=src.rearrange("(p t) j -> p t j", t=4)[:, t0:t1, :],
@@ -122,8 +122,8 @@ def tile_list_gearbox_slot_features_kernel(
         w8d = held("w8d", [P, 2, N], I32)
         for a in range(2):
             nc.vector.tensor_copy(
-                out=w8d[:, a, :].rearrange("p (g t q) -> p g q t", g=2, t=4),
-                in_=w8raw[:, a, :].rearrange("p (g q t) -> p g q t", g=2, t=4),
+                out=w8d[:, a, :].rearrange("p (g t c i) -> p g c t i", g=2, t=4, i=4),
+                in_=w8raw[:, a, :].rearrange("p (g c i t) -> p g c t i", g=2, t=4, i=4),
             )
         vw = held("vw", [P, 2, S], U32)
         vs = held("vs", [P, S], U8)
@@ -131,8 +131,8 @@ def tile_list_gearbox_slot_features_kernel(
         nc.vector.tensor_copy(vs[:], tbs[:].indirect(o1[:]))
         w8sd = held("w8sd", [P, N], U8, "tbs")
         nc.vector.tensor_copy(
-            out=w8sd[:].rearrange("p (g t q) -> p g q t", g=2, t=4),
-            in_=w8s[:].rearrange("p (g q t) -> p g q t", g=2, t=4),
+            out=w8sd[:].rearrange("p (g t c i) -> p g c t i", g=2, t=4, i=16),
+            in_=w8s[:].rearrange("p (g c i t) -> p g c t i", g=2, t=4, i=16),
         )
 
         o4 = load_list("o4", offs4)
@@ -256,8 +256,8 @@ def tile_list_gearbox_slot_features_kernel(
         xs = [held(f"xs{a}", [P, PJ], U8) for a in range(2)]
 
         def weave(engine, dst, src):
-            dst_v = dst.rearrange("p (c i t) -> p c t i", i=4, t=4)
-            src_v = src.rearrange("p t (c i) -> p c t i", i=4)
+            dst_v = dst.rearrange("p (c i t) -> p c t i", i=2, t=4)
+            src_v = src.rearrange("p t (c i) -> p c t i", i=2)
             if engine == "scalar":
                 nc.scalar.copy(out=dst_v, in_=src_v)
             else:

@@ -20,7 +20,11 @@ ALU = mybir.AluOpType
 
 P = 128
 BANK = 512
-VECTOR_SHARE = (0, 192, 192, 352)
+TILES = 8
+LAST = TILES - 1
+AHEAD = 4
+GPSIMD_COLS = 368
+VECTOR_COLS = 288
 ROUNDER = 1.5 * 2.0**23
 
 
@@ -41,52 +45,52 @@ def tile_list_gearbox_slot_features_kernel(
         def ringed(name, shape, dtype, tag):
             return ring.tile(shape, dtype, name=name, tag=tag, align_bytes=64)
 
-        def bank(name, n):
-            return psum.tile([P, BANK], F32, name=name, tag=f"bank{n}")
+        def bank(name, number):
+            return psum.tile([P, BANK], F32, name=name, tag=f"bank{number}")
+
+        def half(c):
+            return slice(c * BANK, (c + 1) * BANK)
 
         def load_list(name, src):
-            t = lists.tile(list(src.shape), U16, name=name)
-            nc.sync.dma_start(t[:], src)
-            return t
+            offsets = lists.tile(list(src.shape), U16, name=name)
+            nc.sync.dma_start(offsets[:], src)
+            return offsets
 
-        def load_words(name, src, tag=None):
-            t = held(name, [P, src.shape[1]], I32, tag)
-            nc.sync.dma_start(out=t[:], in_=src.rearrange("p n t -> p (n t)").bitcast(I32))
-            return t
+        def load_words(name, src):
+            words = held(name, [P, src.shape[1]], I32)
+            nc.sync.dma_start(out=words[:], in_=src.rearrange("p n t -> p (n t)").bitcast(I32))
+            return words
 
         def load_scales(queue, plane, src):
             rows = 4 * src.shape[0]
-            for q in range(4):
+            for quad in range(4):
                 queue.dma_start(
-                    out=plane[32 * q : 32 * q + rows, :].bitcast(I32),
-                    in_=src[:, 4 * q : 4 * q + 4, :].bitcast(I32),
+                    out=plane[32 * quad : 32 * quad + rows, :].bitcast(I32),
+                    in_=src[:, 4 * quad : 4 * quad + 4, :].bitcast(I32),
                 )
 
         def load_page(i):
             b, t = divmod(i, 4)
-            pg = held(f"page{i}", [P, T2], F32)
-            nc.sync.dma_start(out=pg[:], in_=page0.rearrange("(b p t) c -> b t p c", b=2, t=4)[b, t])
-            return pg
+            page = held(f"page{i}", [P, T2], F32)
+            nc.sync.dma_start(out=page[:], in_=page0.rearrange("(b p t) c -> b t p c", b=2, t=4)[b, t])
+            return page
 
         def load_gain(dst, src, t0, t1):
-            for q in (0, 2, 1, 3):
+            for quad in (0, 2, 1, 3):
                 nc.sync.dma_start(
-                    out=dst[32 * q : 32 * q + 32, t0:t1, :],
+                    out=dst[32 * quad : 32 * quad + 32, t0:t1, :],
                     in_=src.rearrange("(p t) j -> p t j", t=4)[:, t0:t1, :],
                 )
 
         def load_w1(a, b, tag):
             raw = held(f"w1raw{a}{b}", [P, 4, BANK], F32, tag)
-            nc.sync.dma_start(
-                out=raw[:],
-                in_=w1[512 * a : 512 * (a + 1), 512 * b : 512 * (b + 1)].rearrange("(p j) c -> p j c", j=4),
-            )
+            nc.sync.dma_start(out=raw[:], in_=w1[half(a), half(b)].rearrange("(p j) c -> p j c", j=4))
             return raw
 
-        def load_vec(name, src):
-            v = held(name, [P, 2, 4], F32)
-            nc.sync.dma_start(out=v[:], in_=src.rearrange("(b p t) -> p b t", b=2, t=4))
-            return v
+        def load_per_row(name, src):
+            values = held(name, [P, 2, 4], F32)
+            nc.sync.dma_start(out=values[:], in_=src.rearrange("(b p t) -> p b t", b=2, t=4))
+            return values[:].rearrange("p b t -> p (b t)")
 
         t2s = held("t2s", [P, TD], U8, "w8d")
         w4s = held("w4s", [P, H], U8)
@@ -94,9 +98,10 @@ def tile_list_gearbox_slot_features_kernel(
         w8s = held("w8s", [P, N], U8)
         nc.vector.memset(t2s[:].bitcast(I32), 0)
         nc.vector.memset(w4s[:].bitcast(I32), 0)
-        warm = held("warm", [P, 4], F32)
-        nc.vector.memset(warm[:, 0:1], 0.0)
-        nc.scalar.activation(out=warm[:, 1:2], in_=warm[:, 0:1], func=ACT.Sin)
+        zeros = held("zeros", [P, 4], F32)
+        sin_bias, gelu_bias, silu_bias = zeros[:, 1:2], zeros[:, 2:3], zeros[:, 3:4]
+        nc.vector.memset(zeros[:, 0:1], 0.0)
+        nc.scalar.activation(out=sin_bias, in_=zeros[:, 0:1], func=ACT.Sin)
         o2 = load_list("o2", offs2)
         t2w = load_words("t2w", tab2_words[0])
         load_scales(nc.sync, t2s, tab2_scales)
@@ -144,9 +149,9 @@ def tile_list_gearbox_slot_features_kernel(
         pages.append(load_page(2))
         tbw.append(load_words("tbw1", tab_words[1]))
         pages.append(load_page(3))
-        lim_v = load_vec("lim_v", lim)
-        gx_v = load_vec("gx_v", gx)
-        gs_v = load_vec("gs_v", gs)
+        lim_r = load_per_row("lim_r", lim)
+        gx_r = load_per_row("gx_r", gx)
+        gs_r = load_per_row("gs_r", gs)
         pages.append(load_page(4))
         pages.append(load_page(5))
         w1raw = {(0, 0): load_w1(0, 0, "big0")}
@@ -168,8 +173,8 @@ def tile_list_gearbox_slot_features_kernel(
                     out=z[:],
                     lhsT=v2w[:, jt * P : (jt + 1) * P].bitcast(FP8X4),
                     lhsT_scale=v2s[:, jt * P : (jt + 1) * P],
-                    rhs=w4w[:, 1024 * b : 1024 * (b + 1)].bitcast(FP4X4),
-                    rhs_scale=w4s[:, 512 * b : 512 * (b + 1)],
+                    rhs=w4w[:, 2 * BANK * b : 2 * BANK * (b + 1)].bitcast(FP4X4),
+                    rhs_scale=w4s[:, half(b)],
                     start=True,
                     stop=True,
                 )
@@ -186,38 +191,34 @@ def tile_list_gearbox_slot_features_kernel(
             t = i % 4
             whole = ringed(f"whole{i}", [P, 4, P], U32, "ka")
             nc.scalar.activation(out=whole[:], in_=u[:, :, t, :], func=ACT.Copy, scale=1.0, bias=ROUNDER)
-            minus = ringed(f"minus{i}", [P, 4, P], F32, "kb")
-            nc.scalar.activation(out=minus[:], in_=whole[:], func=ACT.Copy, scale=-1.0, bias=ROUNDER)
+            minus_whole = ringed(f"minus{i}", [P, 4, P], F32, "kb")
+            nc.scalar.activation(out=minus_whole[:], in_=whole[:], func=ACT.Copy, scale=-1.0, bias=ROUNDER)
             frac = bank(f"frac{i}", 4 + i % 2)
             for jt in range(4):
                 cols = frac[:, jt * P : (jt + 1) * P]
                 nc.tensor.matmul(cols, u[:, jt, t, :], ident[:], start=(jt == 0), stop=False, is_transpose=True)
             for jt in range(4):
                 cols = frac[:, jt * P : (jt + 1) * P]
-                nc.tensor.matmul(cols, minus[:, jt, :], ident[:], start=False, stop=(jt == 3), is_transpose=True)
-            h = held(f"h2_{i}", [P, S], F32, f"h{i}")
-            nc.scalar.activation(out=h[:], in_=frac[:], func=ACT.Sin, scale=2.0 * math.pi)
-            if i == 7:
-                nc.scalar.activation(out=warm[:, 2:3], in_=h[:, 0:1], func=ACT.Gelu_apprx_tanh)
-            return h
+                nc.tensor.matmul(cols, minus_whole[:, jt, :], ident[:], start=False, stop=(jt == 3), is_transpose=True)
+            h2 = held(f"h2_{i}", [P, S], F32, f"h{i}")
+            nc.scalar.activation(out=h2[:], in_=frac[:], func=ACT.Sin, scale=2.0 * math.pi, bias=sin_bias)
+            if i == LAST:
+                nc.scalar.activation(out=gelu_bias, in_=h2[:, 0:1], func=ACT.Gelu_apprx_tanh, scale=0.0)
+            return h2
 
-        def put(i, h, gain, offsets):
-            nc.vector.tensor_tensor(pages[i][:].indirect(offsets[:]), h[:], gain[:, i % 4, :], ALU.mult)
+        def put(i, values, gain, offsets):
+            nc.vector.tensor_tensor(pages[i][:].indirect(offsets[:]), values[:], gain[:, i % 4, :], ALU.mult)
 
         w1c = held("w1c", [P, 2, H], U32)
         w1s = held("w1s", [P, 2, H], U8)
 
-        def round_w1(a, b):
+        def quantise_w1(a, b):
             grouped = ringed(f"w1g{a}{b}", [P, 4 * BANK], BF16, "grp")
             nc.scalar.copy(
                 out=grouped[:].rearrange("p (t m j) -> p m t j", t=4, j=4),
                 in_=w1raw[(a, b)][:].rearrange("p j (m t) -> p m t j", t=4),
             )
-            return grouped
-
-        def quant_w1(a, b, grouped):
-            cols = slice(512 * b, 512 * (b + 1))
-            nc.vector.quantize_mx(out=w1c[:, a, cols].bitcast(FP8X4), scales=w1s[:, a, cols], in_=grouped[:])
+            nc.vector.quantize_mx(out=w1c[:, a, half(b)].bitcast(FP8X4), scales=w1s[:, a, half(b)], in_=grouped[:])
 
         for b in range(2):
             u = turns(b)
@@ -227,11 +228,7 @@ def tile_list_gearbox_slot_features_kernel(
                 if i == 2:
                     nc.vector.tensor_copy(vw[:, 1, :], tbw[1][:].bitcast(U32).indirect(o1[:]))
                 if i in (5, 6):
-                    quant_w1(i - 5, 0, round_w1(i - 5, 0))
-
-        lim_f = lim_v[:].rearrange("p b t -> p (b t)")
-        gx_f = gx_v[:].rearrange("p b t -> p (b t)")
-        gs_f = gs_v[:].rearrange("p b t -> p (b t)")
+                    quantise_w1(i - 5, 0)
 
         def gelu_rows(i):
             vib = bank(f"vib{i}", 6 + i % 2)
@@ -246,105 +243,101 @@ def tile_list_gearbox_slot_features_kernel(
                     start=(a == 0),
                     stop=(a == 1),
                 )
-            h = held(f"h1_{i}", [P, S], F32, f"h{i % 4}")
-            nc.scalar.activation(out=h[:], in_=vib[:], func=ACT.Gelu_apprx_tanh)
-            if i == 7:
-                nc.scalar.activation(out=warm[:, 3:4], in_=h[:, 0:1], func=ACT.Silu)
-            return h
+            h1 = held(f"h1_{i}", [P, S], F32, f"h{i % AHEAD}")
+            nc.scalar.activation(out=h1[:], in_=vib[:], func=ACT.Gelu_apprx_tanh, bias=gelu_bias)
+            if i == LAST:
+                nc.scalar.activation(out=silu_bias, in_=h1[:, 0:1], func=ACT.Silu, scale=0.0)
+            return h1
 
         xc = held("xc", [P, 2 * PJ], U32, "turns0")
         xs = [held(f"xs{a}", [P, PJ], U8) for a in range(2)]
 
-        def weave(engine, dst, src):
-            dst_v = dst.rearrange("p (c i t) -> p c t i", i=2, t=4)
-            src_v = src.rearrange("p t (c i) -> p c t i", i=2)
-            if engine == "scalar":
-                nc.scalar.copy(out=dst_v, in_=src_v)
-            else:
-                nc.vector.tensor_copy(out=dst_v, in_=src_v)
-
-        def quant_x(a, c, woven):
+        def quantise_x(a, c, woven):
             nc.vector.quantize_mx(
                 out=xc[:, a * PJ + c * BANK : a * PJ + (c + 1) * BANK].bitcast(FP8X4),
-                scales=xs[a][:, c * BANK : (c + 1) * BANK],
+                scales=xs[a][:, half(c)],
                 in_=woven,
             )
 
-        def bound_on_scalar(i, got, dsts, floor):
-            nc.scalar.activation(out=got, in_=got, func=ACT.Relu, bias=neg_lim[:, i : i + 1])
-            width = got.shape[1] // len(dsts)
+        def bound_on_scalar(i, picked, dsts, floor):
+            nc.scalar.activation(out=picked, in_=picked, func=ACT.Relu, bias=neg_lim[:, i : i + 1])
+            width = picked.shape[1] // len(dsts)
             for c, dst in enumerate(dsts):
                 nc.scalar.activation(
-                    out=dst, in_=got[:, c * width : (c + 1) * width], func=ACT.Identity,
-                    scale=gx_f[:, i : i + 1], bias=floor[:],
+                    out=dst, in_=picked[:, c * width : (c + 1) * width], func=ACT.Identity,
+                    scale=gx_r[:, i : i + 1], bias=floor[:],
                 )
 
-        def join_pairs(engine, dst, pairs):
-            dst_v = dst.bitcast(F32).rearrange("p (j u) -> p j u", u=2)
-            src_v = pairs.rearrange("p u j e -> p u (j e)").bitcast(F32).rearrange("p u j -> p j u")
-            if engine == "scalar":
-                nc.scalar.copy(out=dst_v, in_=src_v)
-            else:
-                nc.vector.tensor_copy(out=dst_v, in_=src_v)
+        def join_pairs(copy, dst, pairs):
+            copy(
+                out=dst.bitcast(F32).rearrange("p (j u) -> p j u", u=2),
+                in_=pairs.rearrange("p u j e -> p u (j e)").bitcast(F32).rearrange("p u j -> p j u"),
+            )
 
-        h1 = [gelu_rows(i) for i in range(4)]
+        h1 = [gelu_rows(i) for i in range(AHEAD)]
         for a in range(2):
-            quant_w1(a, 1, round_w1(a, 1))
-        xp0_tile = held("xp0", [P, 4 * PJ + 16], BF16, "big3")
+            quantise_w1(a, 1)
+        xp0_tile = held("xp0", [P, 4 * PJ + 2 * TILES], BF16, "big3")
         neg_lim = xp0_tile[:, 4 * PJ :].bitcast(F32)
-        nc.scalar.activation(out=neg_lim, in_=lim_f, func=ACT.Copy, scale=-1.0)
-        neg_gx = held("neg_gx", [P, 8], F32)
-        nc.gpsimd.tensor_scalar(neg_gx[:], gx_f, -1.0, 0.0, ALU.mult, ALU.add)
+        nc.scalar.activation(out=neg_lim, in_=lim_r, func=ACT.Copy, scale=-1.0)
+        neg_gx = held("neg_gx", [P, TILES], F32)
+        nc.gpsimd.tensor_scalar(neg_gx[:], gx_r, -1.0, 0.0, ALU.mult, ALU.add)
         xp0 = xp0_tile[:, : 4 * PJ].rearrange("p (u j e) -> p u j e", u=2, e=2)
         xw0 = held("xw0", [P, 4 * PJ], BF16, "big0")
         xp1 = [held(f"xp1{c}", [P, 2, BANK, 2], BF16, f"big{1 + c}") for c in range(2)]
-        for i in range(7):
+        for i in range(LAST):
             u, e = divmod(i % 4, 2)
             put(i, h1[i], wg1d, o3)
-            floor = held(f"floor{i}", [P, 1], F32, f"h{i % 4}")
+            floor = held(f"floor{i}", [P, 1], F32, f"h{i % AHEAD}")
             nc.scalar.activation(out=floor[:], in_=neg_lim[:, i : i + 1], func=ACT.Copy, scale=neg_gx[:, i : i + 1])
-            got = ringed(f"got{i}", [P, PJ], F32, "got")
-            if i < 6:
-                nc.vector.tensor_copy(got[:], pages[i][:].indirect(o5[:]))
-                bound_on_scalar(i, got[:], [xp0[:, u, :, e]] if i < 4 else [w[:, u, :, e] for w in xp1], floor)
+            picked = ringed(f"got{i}", [P, PJ], F32, "got")
+            if i < LAST - 1:
+                nc.vector.tensor_copy(picked[:], pages[i][:].indirect(o5[:]))
+                dsts = [xp0[:, u, :, e]] if i < 4 else [pairs[:, u, :, e] for pairs in xp1]
+                bound_on_scalar(i, picked[:], dsts, floor)
             else:
                 for c in range(2):
-                    half = got[:, c * BANK : (c + 1) * BANK]
-                    nc.vector.tensor_copy(half, pages[i][:].indirect(o5[:, 32 * c : 32 * (c + 1)]))
-                    bound_on_scalar(i, half, [xp1[c][:, u, :, e]], floor)
-                    nc.scalar.copy(out=got[:, c * BANK : c * BANK + 1], in_=gx_f[:, 7:8])
-            if i < 4:
-                h1.append(gelu_rows(i + 4))
+                    nc.vector.tensor_copy(picked[:, half(c)], pages[i][:].indirect(o5[:, 32 * c : 32 * (c + 1)]))
+                    bound_on_scalar(i, picked[:, half(c)], [xp1[c][:, u, :, e]], floor)
+                    nc.scalar.copy(out=picked[:, c * BANK : c * BANK + 1], in_=gx_r[:, LAST:])
+            if i + AHEAD < TILES:
+                h1.append(gelu_rows(i + AHEAD))
             if i == 3:
                 for c in range(2):
-                    join_pairs("scalar", xw0[:, c * 2048 : (c + 1) * 2048], xp0[:, :, c * BANK : (c + 1) * BANK, :])
-                    quant_x(0, c, xw0[:, c * 2048 : (c + 1) * 2048])
+                    woven = xw0[:, c * 4 * BANK : (c + 1) * 4 * BANK]
+                    join_pairs(nc.scalar.copy, woven, xp0[:, :, half(c), :])
+                    quantise_x(0, c, woven)
 
-        got6 = got
-        put(7, h1[7], wg1d, o3)
+        gx_last = picked
+        put(LAST, h1[LAST], wg1d, o3)
         for c in range(2):
-            got = ringed("got70", [P, BANK], F32, "got") if c == 0 else held("got71", [P, BANK], F32, "tbw1")
-            nc.vector.tensor_copy(got[:], pages[7][:].indirect(o5[:, 32 * c : 32 * (c + 1)]))
+            picked = ringed("got70", [P, BANK], F32, "got") if c == 0 else held("got71", [P, BANK], F32, "tbw1")
+            nc.vector.tensor_copy(picked[:], pages[LAST][:].indirect(o5[:, 32 * c : 32 * (c + 1)]))
             nc.vector.tensor_scalar(
-                xp1[c][:, 1, :, 1], got[:], lim_f[:, 7:8], got6[:, c * BANK : c * BANK + 1], ALU.max, ALU.mult
+                xp1[c][:, 1, :, 1], picked[:], lim_r[:, LAST:], gx_last[:, c * BANK : c * BANK + 1], ALU.max, ALU.mult
             )
             xw1 = held(f"xw1{c}", [P, 4 * BANK], BF16, "tbw1" if c == 0 else "turns1")
-            join_pairs("vector", xw1[:], xp1[c][:])
-            quant_x(1, c, xw1[:])
+            join_pairs(nc.vector.tensor_copy, xw1[:], xp1[c][:])
+            quantise_x(1, c, xw1[:])
 
         yc = held("yc", [P, 2 * PJ], U32, "tbw0")
         ys = held("ys", [P, PJ], U8)
         out_rows = out_0.rearrange("(g p t) j -> g p t j", g=2, t=4)
-        pending = []
 
-        def finish(g, c, woven):
-            cols = slice(c * BANK, (c + 1) * BANK)
-            words = yc[:, g * PJ + c * BANK : g * PJ + (c + 1) * BANK]
-            nc.vector.quantize_mx(out=words.bitcast(FP8X4), scales=ys[4 * g : P, cols], in_=woven[:])
-            nc.sync.dma_start(
-                out=out_1[g].rearrange("p m t -> p (m t)").bitcast(I32)[:, cols], in_=words.bitcast(I32)
+        def weave(copy, dst, src):
+            copy(
+                out=dst.rearrange("p (c i t) -> p c t i", i=2, t=4),
+                in_=src.rearrange("p t (c i) -> p c t i", i=2),
             )
 
+        def quantise_y(g, c, woven):
+            words = yc[:, g * PJ + c * BANK : g * PJ + (c + 1) * BANK]
+            nc.vector.quantize_mx(out=words.bitcast(FP8X4), scales=ys[4 * g : P, half(c)], in_=woven[:])
+            nc.sync.dma_start(
+                out=out_1[g].rearrange("p m t -> p (m t)").bitcast(I32)[:, half(c)], in_=words.bitcast(I32)
+            )
+
+        previous = None
         for c in range(2):
             for g in range(2):
                 y = held(f"y{g}{c}", [P, 4, BANK], F32, f"page{2 * c + g}")
@@ -358,28 +351,36 @@ def tile_list_gearbox_slot_features_kernel(
                             lhsT=w8d[:, a, cols].bitcast(FP8X4),
                             lhsT_scale=w8sd[4 * a : P, cols],
                             rhs=xc[:, a * PJ + c * BANK : a * PJ + (c + 1) * BANK].bitcast(FP8X4),
-                            rhs_scale=xs[a][:, c * BANK : (c + 1) * BANK],
+                            rhs_scale=xs[a][:, half(c)],
                             start=(a == 0),
                             stop=(a == 1),
                         )
-                    if n < 4:
-                        s = ringed(f"silu{c}{n}", [P, BANK], F32, "ka" if n % 2 == 0 else "kb")
+                    if g == 0:
+                        silu = ringed(f"silu{c}{n}", [P, BANK], F32, "ka" if t % 2 == 0 else "kb")
                     else:
-                        s = held(f"silu{c}{n}", [P, BANK], F32, f"h{n - 4}")
-                    nc.scalar.activation(out=s[:], in_=f[:], func=ACT.Silu)
-                    nc.vector.scalar_tensor_tensor(y[:, t, :], s[:], gs_f[:, n : n + 1], f[:], ALU.mult, ALU.add)
-                    nc.sync.dma_start(out=out_rows[g][:, t, c * BANK : (c + 1) * BANK], in_=y[:, t, :])
-                    if t == 1 and pending:
-                        finish(*pending.pop())
-                woven = ringed(f"yw{g}{c}", [P, 4 * BANK], BF16, "grp")
-                share = VECTOR_SHARE[2 * c + g]
-                if share:
-                    weave("vector", woven[:, : 4 * share], y[:, :, :share])
-                weave("scalar", woven[:, 4 * share :], y[:, :, share:])
-                pending.append((g, c, woven))
-        finish(*pending.pop())
-        for q in range(4):
+                        silu = held(f"silu{c}{n}", [P, BANK], F32, f"h{t}")
+                    nc.scalar.activation(out=silu[:], in_=f[:], func=ACT.Silu, bias=silu_bias)
+                    nc.vector.scalar_tensor_tensor(y[:, t, :], silu[:], gs_r[:, n : n + 1], f[:], ALU.mult, ALU.add)
+                    nc.sync.dma_start(out=out_rows[g][:, t, half(c)], in_=y[:, t, :])
+                if previous is not None:
+                    quantise_y(*previous)
+                if c + g < 2:
+                    woven = held(f"yw{g}{c}", [P, 4 * BANK], BF16, "big0")
+                    split = GPSIMD_COLS
+                    nc.gpsimd.tensor_scalar(
+                        woven[:, : 4 * split].rearrange("p (j t) -> p j t", t=4),
+                        y[:, :, :split].rearrange("p t j -> p j t"),
+                        1.0, 0.0, ALU.mult, ALU.add,
+                    )
+                else:
+                    woven = held(f"yw{g}{c}", [P, 4 * BANK], BF16, "big2")
+                    split = VECTOR_COLS
+                    weave(nc.vector.tensor_copy, woven[:, : 4 * split], y[:, :, :split])
+                weave(nc.scalar.copy, woven[:, 4 * split :], y[:, :, split:])
+                previous = (g, c, woven)
+        quantise_y(*previous)
+        for quad in range(4):
             nc.scalar.dma_start(
-                out=out_2[:, 4 * q : 4 * q + 4, :].bitcast(I32),
-                in_=ys[32 * q : 32 * q + 8, :].bitcast(I32),
+                out=out_2[:, 4 * quad : 4 * quad + 4, :].bitcast(I32),
+                in_=ys[32 * quad : 32 * quad + 8, :].bitcast(I32),
             )

import math
from contextlib import ExitStack

import concourse.mybir as mybir
from concourse.masks import make_identity

K, K2, T, TD, S, T2, PJ, H, N = 1024, 512, 2048, 1024, 512, 2048, 1024, 1024, 1024
FLOPS = 2 * (K * H * S + K2 * H * S + H * N * PJ)

F32 = mybir.dt.float32
BF16 = mybir.dt.bfloat16
I32 = mybir.dt.int32
U32 = mybir.dt.uint32
U16 = mybir.dt.uint16
U8 = mybir.dt.uint8
FP8X4 = mybir.dt.float8_e4m3fn_x4
FP4X4 = mybir.dt.float4_e2m1fn_x4
ACT = mybir.ActivationFunctionType
ALU = mybir.AluOpType

P = 128
BANK = 512
TILES = 8
LAST = TILES - 1
AHEAD = 4
GPSIMD_COLS = 368
VECTOR_COLS = 288
ROUNDER = 1.5 * 2.0**23


def tile_list_gearbox_slot_features_kernel(
    tc, tab_words, tab_scales, tab2_words, tab2_scales, offs, offs2, offs3, offs4, offs5,
    w1, w4_words, w4_scales, w8_words, w8_scales, page0, wg1, wg2, lim, gx, gs, out_0, out_1, out_2,
):
    nc = tc.nc
    with ExitStack() as ctx:
        lists = ctx.enter_context(tc.tile_pool(name="lists", bufs=1))
        sb = ctx.enter_context(tc.tile_pool(name="sb", bufs=1))
        ring = ctx.enter_context(tc.tile_pool(name="ring", bufs=2))
        psum = ctx.enter_context(tc.psum_pool(name="psum", bufs=1))

        def held(name, shape, dtype, tag=None):
            return sb.tile(shape, dtype, name=name, tag=tag or name, align_bytes=64)

        def ringed(name, shape, dtype, tag):
            return ring.tile(shape, dtype, name=name, tag=tag, align_bytes=64)

        def bank(name, number):
            return psum.tile([P, BANK], F32, name=name, tag=f"bank{number}")

        def half(c):
            return slice(c * BANK, (c + 1) * BANK)

        def load_list(name, src):
            offsets = lists.tile(list(src.shape), U16, name=name)
            nc.sync.dma_start(offsets[:], src)
            return offsets

        def load_words(name, src):
            words = held(name, [P, src.shape[1]], I32)
            nc.sync.dma_start(out=words[:], in_=src.rearrange("p n t -> p (n t)").bitcast(I32))
            return words

        def load_scales(queue, plane, src):
            rows = 4 * src.shape[0]
            for quad in range(4):
                queue.dma_start(
                    out=plane[32 * quad : 32 * quad + rows, :].bitcast(I32),
                    in_=src[:, 4 * quad : 4 * quad + 4, :].bitcast(I32),
                )

        def load_page(i):
            b, t = divmod(i, 4)
            page = held(f"page{i}", [P, T2], F32)
            nc.sync.dma_start(out=page[:], in_=page0.rearrange("(b p t) c -> b t p c", b=2, t=4)[b, t])
            return page

        def load_gain(dst, src, t0, t1):
            for quad in (0, 2, 1, 3):
                nc.sync.dma_start(
                    out=dst[32 * quad : 32 * quad + 32, t0:t1, :],
                    in_=src.rearrange("(p t) j -> p t j", t=4)[:, t0:t1, :],
                )

        def load_w1(a, b, tag):
            raw = held(f"w1raw{a}{b}", [P, 4, BANK], F32, tag)
            nc.sync.dma_start(out=raw[:], in_=w1[half(a), half(b)].rearrange("(p j) c -> p j c", j=4))
            return raw

        def load_per_row(name, src):
            values = held(name, [P, 2, 4], F32)
            nc.sync.dma_start(out=values[:], in_=src.rearrange("(b p t) -> p b t", b=2, t=4))
            return values[:].rearrange("p b t -> p (b t)")

        t2s = held("t2s", [P, TD], U8, "w8d")
        w4s = held("w4s", [P, H], U8)
        tbs = held("tbs", [P, T], U8)
        w8s = held("w8s", [P, N], U8)
        nc.vector.memset(t2s[:].bitcast(I32), 0)
        nc.vector.memset(w4s[:].bitcast(I32), 0)
        zeros = held("zeros", [P, 4], F32)
        sin_bias, gelu_bias, silu_bias = zeros[:, 1:2], zeros[:, 2:3], zeros[:, 3:4]
        nc.vector.memset(zeros[:, 0:1], 0.0)
        nc.scalar.activation(out=sin_bias, in_=zeros[:, 0:1], func=ACT.Sin)
        o2 = load_list("o2", offs2)
        t2w = load_words("t2w", tab2_words[0])
        load_scales(nc.sync, t2s, tab2_scales)
        w4w = held("w4w", [P, 2 * H], U8)
        nc.sync.dma_start(out=w4w[:].bitcast(I32), in_=w4_words[0].bitcast(I32))
        w8raw = held("w8raw", [P, 2, N], I32, "big3")
        nc.sync.dma_start(out=w8raw[:], in_=w8_words.rearrange("a p n t -> p a (n t)").bitcast(I32))
        load_scales(nc.sync, w4s, w4_scales)
        nc.vector.memset(tbs[:].bitcast(I32), 0)
        nc.gpsimd.memset(w8s[:].bitcast(I32), 0)
        load_scales(nc.gpsimd, w8s, w8_scales)
        ident = held("ident", [P, P], F32)
        make_identity(nc, ident[:])
        o1 = load_list("o1", offs)
        tbw = [load_words("tbw0", tab_words[0])]
        load_scales(nc.sync, tbs, tab_scales)

        v2w = held("v2w", [P, S], U32)
        v2s = held("v2s", [P, S], U8)
        nc.vector.tensor_copy(v2w[:], t2w[:].bitcast(U32).indirect(o2[:]))
        nc.vector.tensor_copy(v2s[:], t2s[:].indirect(o2[:]))

        w8d = held("w8d", [P, 2, N], I32)
        for a in range(2):
            nc.vector.tensor_copy(
                out=w8d[:, a, :].rearrange("p (g t c i) -> p g c t i", g=2, t=4, i=4),
                in_=w8raw[:, a, :].rearrange("p (g c i t) -> p g c t i", g=2, t=4, i=4),
            )
        vw = held("vw", [P, 2, S], U32)
        vs = held("vs", [P, S], U8)
        nc.vector.tensor_copy(vw[:, 0, :], tbw[0][:].bitcast(U32).indirect(o1[:]))
        nc.vector.tensor_copy(vs[:], tbs[:].indirect(o1[:]))
        w8sd = held("w8sd", [P, N], U8, "tbs")
        nc.vector.tensor_copy(
            out=w8sd[:].rearrange("p (g t c i) -> p g c t i", g=2, t=4, i=16),
            in_=w8s[:].rearrange("p (g c i t) -> p g c t i", g=2, t=4, i=16),
        )

        o4 = load_list("o4", offs4)
        wg2d = held("wg2d", [P, 4, S], F32)
        wg1d = held("wg1d", [P, 4, S], F32)
        load_gain(wg2d, wg2, 0, 2)
        pages = [load_page(0), load_page(1)]
        load_gain(wg2d, wg2, 2, 4)
        pages.append(load_page(2))
        tbw.append(load_words("tbw1", tab_words[1]))
        pages.append(load_page(3))
        lim_r = load_per_row("lim_r", lim)
        gx_r = load_per_row("gx_r", gx)
        gs_r = load_per_row("gs_r", gs)
        pages.append(load_page(4))
        pages.append(load_page(5))
        w1raw = {(0, 0): load_w1(0, 0, "big0")}
        w1raw[(1, 0)] = load_w1(1, 0, "big1")
        pages.append(load_page(6))
        pages.append(load_page(7))
        o3 = load_list("o3", offs3)
        o5 = load_list("o5", offs5)
        load_gain(wg1d, wg1, 0, 2)
        w1raw[(0, 1)] = load_w1(0, 1, "big2")
        load_gain(wg1d, wg1, 2, 4)
        w1raw[(1, 1)] = load_w1(1, 1, "big3")

        def turns(b):
            u = held(f"turns{b}", [P, 4, 4, P], F32)
            for jt in range(4):
                z = bank(f"z{b}{jt}", jt)
                nc.tensor.matmul_mx(
                    out=z[:],
                    lhsT=v2w[:, jt * P : (jt + 1) * P].bitcast(FP8X4),
                    lhsT_scale=v2s[:, jt * P : (jt + 1) * P],
                    rhs=w4w[:, 2 * BANK * b : 2 * BANK * (b + 1)].bitcast(FP4X4),
                    rhs_scale=w4s[:, half(b)],
                    start=True,
                    stop=True,
                )
                nc.scalar.activation(
                    out=u[:, jt, :, :],
                    in_=z[:].rearrange("p (q t) -> p t q", t=4),
                    func=ACT.Copy,
                    scale=1.0 / (2.0 * math.pi),
                    bias=0.25,
                )
            return u

        def cos_rows(i, u):
            t = i % 4
            whole = ringed(f"whole{i}", [P, 4, P], U32, "ka")
            nc.scalar.activation(out=whole[:], in_=u[:, :, t, :], func=ACT.Copy, scale=1.0, bias=ROUNDER)
            minus_whole = ringed(f"minus{i}", [P, 4, P], F32, "kb")
            nc.scalar.activation(out=minus_whole[:], in_=whole[:], func=ACT.Copy, scale=-1.0, bias=ROUNDER)
            frac = bank(f"frac{i}", 4 + i % 2)
            for jt in range(4):
                cols = frac[:, jt * P : (jt + 1) * P]
                nc.tensor.matmul(cols, u[:, jt, t, :], ident[:], start=(jt == 0), stop=False, is_transpose=True)
            for jt in range(4):
                cols = frac[:, jt * P : (jt + 1) * P]
                nc.tensor.matmul(cols, minus_whole[:, jt, :], ident[:], start=False, stop=(jt == 3), is_transpose=True)
            h2 = held(f"h2_{i}", [P, S], F32, f"h{i}")
            nc.scalar.activation(out=h2[:], in_=frac[:], func=ACT.Sin, scale=2.0 * math.pi, bias=sin_bias)
            if i == LAST:
                nc.scalar.activation(out=gelu_bias, in_=h2[:, 0:1], func=ACT.Gelu_apprx_tanh, scale=0.0)
            return h2

        def put(i, values, gain, offsets):
            nc.vector.tensor_tensor(pages[i][:].indirect(offsets[:]), values[:], gain[:, i % 4, :], ALU.mult)

        w1c = held("w1c", [P, 2, H], U32)
        w1s = held("w1s", [P, 2, H], U8)

        def quantise_w1(a, b):
            grouped = ringed(f"w1g{a}{b}", [P, 4 * BANK], BF16, "grp")
            nc.scalar.copy(
                out=grouped[:].rearrange("p (t m j) -> p m t j", t=4, j=4),
                in_=w1raw[(a, b)][:].rearrange("p j (m t) -> p m t j", t=4),
            )
            nc.vector.quantize_mx(out=w1c[:, a, half(b)].bitcast(FP8X4), scales=w1s[:, a, half(b)], in_=grouped[:])

        for b in range(2):
            u = turns(b)
            for t in range(4):
                i = 4 * b + t
                put(i, cos_rows(i, u), wg2d, o4)
                if i == 2:
                    nc.vector.tensor_copy(vw[:, 1, :], tbw[1][:].bitcast(U32).indirect(o1[:]))
                if i in (5, 6):
                    quantise_w1(i - 5, 0)

        def gelu_rows(i):
            vib = bank(f"vib{i}", 6 + i % 2)
            cols = slice(P * i, P * (i + 1))
            for a in range(2):
                nc.tensor.matmul_mx(
                    out=vib[:],
                    lhsT=w1c[:, a, cols].bitcast(FP8X4),
                    lhsT_scale=w1s[:, a, cols],
                    rhs=vw[:, a, :].bitcast(FP8X4),
                    rhs_scale=vs[4 * a : P, :],
                    start=(a == 0),
                    stop=(a == 1),
                )
            h1 = held(f"h1_{i}", [P, S], F32, f"h{i % AHEAD}")
            nc.scalar.activation(out=h1[:], in_=vib[:], func=ACT.Gelu_apprx_tanh, bias=gelu_bias)
            if i == LAST:
                nc.scalar.activation(out=silu_bias, in_=h1[:, 0:1], func=ACT.Silu, scale=0.0)
            return h1

        xc = held("xc", [P, 2 * PJ], U32, "turns0")
        xs = [held(f"xs{a}", [P, PJ], U8) for a in range(2)]

        def quantise_x(a, c, woven):
            nc.vector.quantize_mx(
                out=xc[:, a * PJ + c * BANK : a * PJ + (c + 1) * BANK].bitcast(FP8X4),
                scales=xs[a][:, half(c)],
                in_=woven,
            )

        def bound_on_scalar(i, picked, dsts, floor):
            nc.scalar.activation(out=picked, in_=picked, func=ACT.Relu, bias=neg_lim[:, i : i + 1])
            width = picked.shape[1] // len(dsts)
            for c, dst in enumerate(dsts):
                nc.scalar.activation(
                    out=dst, in_=picked[:, c * width : (c + 1) * width], func=ACT.Identity,
                    scale=gx_r[:, i : i + 1], bias=floor[:],
                )

        def join_pairs(copy, dst, pairs):
            copy(
                out=dst.bitcast(F32).rearrange("p (j u) -> p j u", u=2),
                in_=pairs.rearrange("p u j e -> p u (j e)").bitcast(F32).rearrange("p u j -> p j u"),
            )

        h1 = [gelu_rows(i) for i in range(AHEAD)]
        for a in range(2):
            quantise_w1(a, 1)
        xp0_tile = held("xp0", [P, 4 * PJ + 2 * TILES], BF16, "big3")
        neg_lim = xp0_tile[:, 4 * PJ :].bitcast(F32)
        nc.scalar.activation(out=neg_lim, in_=lim_r, func=ACT.Copy, scale=-1.0)
        neg_gx = held("neg_gx", [P, TILES], F32)
        nc.gpsimd.tensor_scalar(neg_gx[:], gx_r, -1.0, 0.0, ALU.mult, ALU.add)
        xp0 = xp0_tile[:, : 4 * PJ].rearrange("p (u j e) -> p u j e", u=2, e=2)
        xw0 = held("xw0", [P, 4 * PJ], BF16, "big0")
        xp1 = [held(f"xp1{c}", [P, 2, BANK, 2], BF16, f"big{1 + c}") for c in range(2)]
        for i in range(LAST):
            u, e = divmod(i % 4, 2)
            put(i, h1[i], wg1d, o3)
            floor = held(f"floor{i}", [P, 1], F32, f"h{i % AHEAD}")
            nc.scalar.activation(out=floor[:], in_=neg_lim[:, i : i + 1], func=ACT.Copy, scale=neg_gx[:, i : i + 1])
            picked = ringed(f"got{i}", [P, PJ], F32, "got")
            if i < LAST - 1:
                nc.vector.tensor_copy(picked[:], pages[i][:].indirect(o5[:]))
                dsts = [xp0[:, u, :, e]] if i < 4 else [pairs[:, u, :, e] for pairs in xp1]
                bound_on_scalar(i, picked[:], dsts, floor)
            else:
                for c in range(2):
                    nc.vector.tensor_copy(picked[:, half(c)], pages[i][:].indirect(o5[:, 32 * c : 32 * (c + 1)]))
                    bound_on_scalar(i, picked[:, half(c)], [xp1[c][:, u, :, e]], floor)
                    nc.scalar.copy(out=picked[:, c * BANK : c * BANK + 1], in_=gx_r[:, LAST:])
            if i + AHEAD < TILES:
                h1.append(gelu_rows(i + AHEAD))
            if i == 3:
                for c in range(2):
                    woven = xw0[:, c * 4 * BANK : (c + 1) * 4 * BANK]
                    join_pairs(nc.scalar.copy, woven, xp0[:, :, half(c), :])
                    quantise_x(0, c, woven)

        gx_last = picked
        put(LAST, h1[LAST], wg1d, o3)
        for c in range(2):
            picked = ringed("got70", [P, BANK], F32, "got") if c == 0 else held("got71", [P, BANK], F32, "tbw1")
            nc.vector.tensor_copy(picked[:], pages[LAST][:].indirect(o5[:, 32 * c : 32 * (c + 1)]))
            nc.vector.tensor_scalar(
                xp1[c][:, 1, :, 1], picked[:], lim_r[:, LAST:], gx_last[:, c * BANK : c * BANK + 1], ALU.max, ALU.mult
            )
            xw1 = held(f"xw1{c}", [P, 4 * BANK], BF16, "tbw1" if c == 0 else "turns1")
            join_pairs(nc.vector.tensor_copy, xw1[:], xp1[c][:])
            quantise_x(1, c, xw1[:])

        yc = held("yc", [P, 2 * PJ], U32, "tbw0")
        ys = held("ys", [P, PJ], U8)
        out_rows = out_0.rearrange("(g p t) j -> g p t j", g=2, t=4)

        def weave(copy, dst, src):
            copy(
                out=dst.rearrange("p (c i t) -> p c t i", i=2, t=4),
                in_=src.rearrange("p t (c i) -> p c t i", i=2),
            )

        def quantise_y(g, c, woven):
            words = yc[:, g * PJ + c * BANK : g * PJ + (c + 1) * BANK]
            nc.vector.quantize_mx(out=words.bitcast(FP8X4), scales=ys[4 * g : P, half(c)], in_=woven[:])
            nc.sync.dma_start(
                out=out_1[g].rearrange("p m t -> p (m t)").bitcast(I32)[:, half(c)], in_=words.bitcast(I32)
            )

        previous = None
        for c in range(2):
            for g in range(2):
                y = held(f"y{g}{c}", [P, 4, BANK], F32, f"page{2 * c + g}")
                for t in range(4):
                    n = 4 * g + t
                    f = bank(f"f{c}{n}", n)
                    cols = slice(P * n, P * (n + 1))
                    for a in range(2):
                        nc.tensor.matmul_mx(
                            out=f[:],
                            lhsT=w8d[:, a, cols].bitcast(FP8X4),
                            lhsT_scale=w8sd[4 * a : P, cols],
                            rhs=xc[:, a * PJ + c * BANK : a * PJ + (c + 1) * BANK].bitcast(FP8X4),
                            rhs_scale=xs[a][:, half(c)],
                            start=(a == 0),
                            stop=(a == 1),
                        )
                    if g == 0:
                        silu = ringed(f"silu{c}{n}", [P, BANK], F32, "ka" if t % 2 == 0 else "kb")
                    else:
                        silu = held(f"silu{c}{n}", [P, BANK], F32, f"h{t}")
                    nc.scalar.activation(out=silu[:], in_=f[:], func=ACT.Silu, bias=silu_bias)
                    nc.vector.scalar_tensor_tensor(y[:, t, :], silu[:], gs_r[:, n : n + 1], f[:], ALU.mult, ALU.add)
                    nc.sync.dma_start(out=out_rows[g][:, t, half(c)], in_=y[:, t, :])
                if previous is not None:
                    quantise_y(*previous)
                if c + g < 2:
                    woven = held(f"yw{g}{c}", [P, 4 * BANK], BF16, "big0")
                    split = GPSIMD_COLS
                    nc.gpsimd.tensor_scalar(
                        woven[:, : 4 * split].rearrange("p (j t) -> p j t", t=4),
                        y[:, :, :split].rearrange("p t j -> p j t"),
                        1.0, 0.0, ALU.mult, ALU.add,
                    )
                else:
                    woven = held(f"yw{g}{c}", [P, 4 * BANK], BF16, "big2")
                    split = VECTOR_COLS
                    weave(nc.vector.tensor_copy, woven[:, : 4 * split], y[:, :, :split])
                weave(nc.scalar.copy, woven[:, 4 * split :], y[:, :, split:])
                previous = (g, c, woven)
        quantise_y(*previous)
        for quad in range(4):
            nc.scalar.dma_start(
                out=out_2[:, 4 * quad : 4 * quad + 4, :].bitcast(I32),
                in_=ys[32 * quad : 32 * quad + 8, :].bitcast(I32),
            )
